import numpy as np
import ml_dtypes


def mxq(x, axis, fmt="e4m3"):
    dtype, down = {"e4m3": (ml_dtypes.float8_e4m3fn, 7), "e5m2": (ml_dtypes.float8_e5m2, 14)}[fmt]
    v = np.moveaxis(np.asarray(x, np.float32).astype(ml_dtypes.bfloat16).astype(np.float64), axis, -1)
    blocks = v.reshape(v.shape[:-1] + (-1, 32))
    amax = np.abs(blocks).max(-1, keepdims=True)
    byte = np.maximum(np.where(amax > 0, np.frexp(amax)[1] - 1 + 127, 0) - down, 1)
    scale = np.exp2(byte - 127.0)
    codes = (blocks / scale).astype(np.float32).astype(dtype).astype(np.float64)
    return np.moveaxis((codes * scale).reshape(v.shape), -1, axis)


WIDE = False


def mx_kscale(k):
    if not WIDE:
        return np.ones(k)
    levels = np.array([10, -10, 5, -5, 0])
    if k % 512:
        return np.exp2(np.random.permutation(np.resize(levels, k // 32))).repeat(32)
    a = np.empty((k // 512, 16))
    for p in range(k // 512):
        a[p, :8] = np.random.permutation(np.resize(levels, 8))
        for g in range(8):
            far = levels[np.abs(levels - a[p, g]) >= 10]
            a[p, g + 8] = far[np.random.randint(len(far))]
    return np.exp2(a.ravel()).repeat(32)


def f64(x):
    return np.asarray(x).astype(np.float64)


def striped(idx):
    return np.tile(idx.reshape(-1, 16).T, (8, 1)).astype(np.uint16)


def unstriped(offs):
    return offs[:16].T.reshape(-1).astype(np.int64)


def striped8(idx):
    return np.concatenate([x.reshape(-1, 16).T for x in idx]).astype(np.uint16)


def runs(offs, k):
    lists = np.stack([offs[16 * r : 16 * r + 16].T.reshape(-1) for r in range(8)]).astype(np.int64)
    return lists[np.arange(k) % 512 // 64]


def pack_weight(w):
    k, n = w.shape
    w = f64(np.asarray(w, np.float32).astype(ml_dtypes.bfloat16)).reshape(k // 32, 32, n)
    amax = np.abs(w).max(1)
    byte = np.clip(np.where(amax > 0, np.frexp(amax)[1] - 1 + 127 - 7, 1), 1, 254)
    scaled = (w * np.exp2(127.0 - byte)[:, None, :]).reshape(k, n).astype(np.float32)
    words = np.ascontiguousarray(scaled.reshape(k // 512, 128, 4, n).transpose(0, 1, 3, 2)).astype(ml_dtypes.float8_e4m3fn).view(np.uint8)
    return words, np.ascontiguousarray(byte.astype(np.uint8).reshape(k // 512, 16, n))


def unpack_weight(words, scales):
    g, p, n, _ = words.shape
    vals = np.ascontiguousarray(words).view(ml_dtypes.float8_e4m3fn).astype(np.float64) * np.repeat(np.exp2(scales.astype(np.float64) - 127.0), 8, axis=1)[..., None]
    return vals.transpose(0, 1, 3, 2).reshape(g * 512, n)


K, T, S, G, H, C, U = 512, 1024, 256, 2048, 512, 512, 512


def setup_inputs():
    n = np.random.standard_normal
    s = mx_kscale(K)[:, None]
    packed_xT = pack_weight(n((K, T)) * s)
    packed_dT = pack_weight(n((K, G)) / s)
    perm = np.random.permutation(U)
    return {
        "x_words": packed_xT[0],
        "x_scales": packed_xT[1],
        "d_words": packed_dT[0],
        "d_scales": packed_dT[1],
        "gs": (np.random.uniform(0.5, 1.5, (K, 1)) / s).astype(np.float32),
        "offs": striped(np.random.permutation(T)[:S]),
        "k1": striped8(np.random.randint(0, G, (8, H))),
        "n1": striped(np.random.permutation(S)),
        "n2": striped(np.random.permutation(S)),
        "cand": striped8(np.random.randint(0, T, (8, C))),
        "n3": striped(perm[:S]),
        "n4": striped(perm[S:]),
        "n5": striped(np.random.permutation(S)),
    }


def reference(x_words, x_scales, d_words, d_scales, gs, offs, k1, n1, n2, cand, n3, n4, n5):
    x_cand = unpack_weight(x_words, x_scales)[np.arange(K)[:, None], runs(cand, K)]
    d_k1 = unpack_weight(d_words, d_scales)[np.arange(K)[:, None], runs(k1, K)]
    xq = unpack_weight(x_words, x_scales)[:, unstriped(offs)]
    h = 0.0625 * (d_k1.T @ xq)
    ds = np.zeros((H, S))
    ds[:, unstriped(n1)] = h
    z = f64(gs) * (np.maximum(h, ds[:, unstriped(n2)]))
    s = 0.0625 * ((x_cand.T @ mxq(z, 0, "e4m3")))
    nw = s - s[:, unstriped(n5)]
    ph = np.zeros((C, U))
    ph[:, unstriped(n3)] = s
    out = ph.copy()
    out[:, unstriped(n4)] = nw
    return out

@@ -1,0 +1,207 @@
+from contextlib import ExitStack
+
+import concourse.mybir as mybir
+
+K, T, S, G, H, C, U = 512, 1024, 256, 2048, 512, 512, 512
+FLOPS = 2 * K * H * S + 2 * K * C * S
+
+F32 = mybir.dt.float32
+BF16 = mybir.dt.bfloat16
+I32 = mybir.dt.int32
+U32 = mybir.dt.uint32
+U16 = mybir.dt.uint16
+U8 = mybir.dt.uint8
+FP8X4 = mybir.dt.float8_e4m3fn_x4
+COPY = mybir.ActivationFunctionType.Copy
+ALU = mybir.AluOpType
+
+P = 128
+PACK = 4
+GROUP = 16
+QUAD = 32
+TILES = 4
+CHUNKS = ((0, 64), (64, 128), (128, 256))
+DS_WIDTH = 384
+S_WIDTH = S + 8
+SIXTEENTH = 0.0625
+
+
+def tile_picked_pqhcrelaypagq_none_p_kernel(
+    tc, x_words, x_scales, d_words, d_scales, gs, offs, k1, n1, n2, cand, n3, n4, n5, out
+):
+    nc = tc.nc
+    with ExitStack() as ctx:
+        lists = ctx.enter_context(tc.tile_pool(name="lists", bufs=1))
+        keep = ctx.enter_context(tc.tile_pool(name="keep", bufs=1))
+        psum = ctx.enter_context(tc.psum_pool(name="psum", bufs=1))
+
+        def load_list(name, src):
+            tile = lists.tile(list(src.shape), U16, name=name)
+            nc.sync.dma_start(tile[:], src)
+            return tile
+
+        def load_words(name, src, width):
+            tile = keep.tile([P, width], U32, name=name, align_bytes=64)
+            nc.sync.dma_start(tile[:].bitcast(I32), src[0].rearrange("p n t -> p (n t)").bitcast(I32))
+            return tile
+
+        def load_scale_rows(queue, table, rows, first, step):
+            n = rows.shape[1]
+            picked = rows[first:16:step, :]
+            count = picked.shape[0]
+            queue.dma_start(
+                table[first:P:step, :].bitcast(I32),
+                picked.unsqueeze(1).to_broadcast([count, P // step // count, n]),
+            )
+
+        def place_odd_rows(dst, src):
+            for c, queue in enumerate((nc.scalar, nc.scalar)):
+                queue.dma_start(dst[2 + c : P : QUAD, :].bitcast(I32), src[GROUP + c : P : QUAD, :].bitcast(I32))
+
+        def place_odd_rows4(dst, src):
+            for c, queue in enumerate((nc.sync, nc.sync)):
+                queue.dma_start(dst[2 + c : P : QUAD, :].bitcast(I32), src[GROUP + 2 + c : P : QUAD, :].bitcast(I32))
+
+        d_byte_table = keep.tile([P, G], U8, name="d_byte_table", align_bytes=64)
+        x_byte_table = keep.tile([P, T], U8, name="x_byte_table", align_bytes=64)
+        d_rows = d_scales[0].bitcast(I32)
+        x_rows = x_scales[0].bitcast(I32)
+        k1_list = load_list("k1_list", k1)
+        load_scale_rows(nc.scalar, d_byte_table, d_rows, 0, 2)
+        load_scale_rows(nc.sync, d_byte_table, d_rows, 1, 2)
+        offs_list = load_list("offs_list", offs)
+        d_word_table = load_words("d_word_table", d_words, G)
+        x_word_table = load_words("x_word_table", x_words, T)
+        for r in range(4):
+            load_scale_rows(nc.scalar, x_byte_table, x_rows, r, 4)
+        n1_list = load_list("n1_list", n1)
+        cand_list = load_list("cand_list", cand)
+        n2_list = load_list("n2_list", n2)
+        n3_list = load_list("n3_list", n3)
+        n5_list = load_list("n5_list", n5)
+        n4_list = load_list("n4_list", n4)
+        gain = keep.tile([P, PACK], F32, name="gain")
+        nc.gpsimd.dma_start(gain[:], gs.rearrange("(p t) o -> p (t o)", t=PACK))
+
+        s_rows = []
+        for u in range(TILES):
+            s_row = keep.tile([P, S_WIDTH], F32, name="s_row%d" % u)
+            nc.gpsimd.memset(s_row[:, S:], 0.0)
+            s_rows.append(s_row)
+
+        d_bytes = keep.tile([P, H], U8, name="d_bytes", align_bytes=64)
+        nc.vector.tensor_copy(d_bytes[:], d_byte_table[:].indirect(k1_list[:]))
+        d_plane = keep.tile([P, H], U8, name="d_plane", tag="d_plane", align_bytes=64)
+        nc.vector.tensor_copy(
+            d_plane[:].rearrange("p (t m) -> p m t", t=PACK),
+            d_bytes[:].rearrange("p (m t) -> p m t", t=PACK),
+        )
+        place_odd_rows(d_plane, d_plane)
+        q_plane = keep.tile([P, S], U8, name="q_plane", align_bytes=64)
+        nc.vector.tensor_copy(q_plane[:], x_byte_table[:].indirect(offs_list[:]))
+        d_picked = keep.tile([P, H], U32, name="d_picked", tag="picked", align_bytes=64)
+        nc.vector.tensor_copy(d_picked[:], d_word_table[:].indirect(k1_list[:]))
+        d_codes = keep.tile([P, H], U32, name="d_codes", tag="stationary", align_bytes=64)
+        nc.vector.tensor_copy(
+            d_codes[:].rearrange("p (t m) -> p m t", t=PACK),
+            d_picked[:].rearrange("p (m t) -> p m t", t=PACK),
+        )
+        q_codes = keep.tile([P, S], U32, name="q_codes", tag="picked", align_bytes=64)
+        nc.vector.tensor_copy(q_codes[:], x_word_table[:].indirect(offs_list[:]))
+
+        h_sums = []
+        ds_rows = []
+        lead = CHUNKS[0][1]
+        gots = {}
+
+        def fetch_ds(dst, t, lo, hi):
+            nc.scalar.activation(dst, ds_rows[t][:, :S].indirect(n2_list[:, lo // GROUP : hi // GROUP]), COPY)
+
+        for t in range(TILES):
+            cols = slice(P * t, P * (t + 1))
+            h_sum = psum.tile([P, S], F32, name="h_sum%d" % t)
+            nc.tensor.matmul_mx(
+                out=h_sum[:],
+                lhsT=d_codes[:, cols].bitcast(FP8X4),
+                lhsT_scale=d_plane[:, cols],
+                rhs=q_codes[:].bitcast(FP8X4),
+                rhs_scale=q_plane[:],
+                start=True,
+                stop=True,
+            )
+            h_row = keep.tile([P, S], F32, name="h_row%d" % t, tag="h_row%d" % t)
+            nc.vector.tensor_scalar(h_row[:], h_sum[:], SIXTEENTH, None, ALU.mult)
+            ds_row = keep.tile([P, DS_WIDTH], F32, name="ds_row%d" % t)
+            nc.scalar.activation(ds_row[:].indirect(n1_list[:]), h_row[:], COPY)
+            h_sums.append(h_sum)
+            ds_rows.append(ds_row)
+            if 0 < t < TILES - 1:
+                early = keep.tile([P, lead], F32, name="early%d" % t, tag="h_row%d" % t)
+                fetch_ds(early[:], t - 1, 0, lead)
+                gots[(t - 1, 0)] = early[:]
+        late = keep.tile([P, TILES, S], F32, name="late", tag="h_row%d" % (TILES - 1))
+        for lo, hi in CHUNKS:
+            for t in range(TILES):
+                if (t, lo) not in gots:
+                    fetch_ds(late[:, t, lo:hi], t, lo, hi)
+                    gots[(t, lo)] = late[:, t, lo:hi]
+
+        cand_bytes = keep.tile([P, C], U8, name="cand_bytes", tag="d_plane", align_bytes=64)
+        nc.vector.tensor_copy(cand_bytes[:], x_byte_table[:].indirect(cand_list[:]))
+        cand_plane = keep.tile([P, C], U8, name="cand_plane", align_bytes=64)
+        nc.vector.tensor_copy(cand_plane[:].bitcast(I32), cand_bytes[:].bitcast(I32))
+        place_odd_rows4(cand_plane, cand_bytes)
+        cand_codes = keep.tile([P, C], U32, name="cand_codes", tag="stationary", align_bytes=64)
+        nc.vector.tensor_copy(cand_codes[:], x_word_table[:].indirect(cand_list[:]))
+
+        s_sums = [psum.tile([P, S], F32, name="s_sum%d" % u) for u in range(TILES)]
+        pages = [keep.tile([P, U], F32, name="page%d" % u) for u in range(TILES)]
+        for lo, hi in CHUNKS:
+            cols = slice(lo, hi)
+            width = hi - lo
+            larger = keep.tile([P, TILES, width], F32, name="larger%d" % lo)
+            z = keep.tile([P, width, PACK], BF16, name="z%d" % lo, align_bytes=64)
+            for pair in ((0, 1), (2, 3)):
+                for t in pair:
+                    nc.vector.scalar_tensor_tensor(
+                        larger[:, t, :], h_sums[t][:, cols], SIXTEENTH, gots[(t, lo)], ALU.mult, ALU.max
+                    )
+                for t in pair:
+                    nc.vector.tensor_scalar(z[:, :, t], larger[:, t, :], gain[:, t : t + 1], None, ALU.mult)
+            z_codes = keep.tile([P, width], U32, name="z_codes%d" % lo, align_bytes=64)
+            z_plane = keep.tile([P, width], U8, name="z_plane%d" % lo, align_bytes=64)
+            nc.vector.quantize_mx(
+                out=z_codes[:].bitcast(FP8X4), scales=z_plane[:], in_=z[:].rearrange("p j t -> p (j t)")
+            )
+            for u in range(TILES):
+                rows = slice(P * u, P * (u + 1))
+                nc.tensor.matmul_mx(
+                    out=s_sums[u][:, cols],
+                    lhsT=cand_codes[:, rows].bitcast(FP8X4),
+                    lhsT_scale=cand_plane[:, rows],
+                    rhs=z_codes[:].bitcast(FP8X4),
+                    rhs_scale=z_plane[:],
+                    start=True,
+                    stop=True,
+                )
+                nc.vector.tensor_scalar(s_rows[u][:, cols], s_sums[u][:, cols], SIXTEENTH, None, ALU.mult)
+
+        def put_s(u, lo, hi):
+            nc.scalar.activation(pages[u][:].indirect(n3_list[:, lo // GROUP : hi // GROUP]), s_rows[u][:, lo:hi], COPY)
+
+        for lo, hi in CHUNKS[:-1]:
+            for u in range(TILES):
+                put_s(u, lo, hi)
+        nws = []
+        for u in range(TILES):
+            other = keep.tile([P, S], F32, name="other%d" % u)
+            nc.scalar.activation(other[:], s_rows[u][:].indirect(n5_list[:]), COPY)
+            nw = keep.tile([P, S], F32, name="nw%d" % u)
+            nc.vector.tensor_tensor(nw[:], s_rows[u][:, :S], other[:], ALU.subtract)
+            nws.append(nw)
+            put_s(u, CHUNKS[-1][0], CHUNKS[-1][1])
+            if u > 0:
+                nc.scalar.activation(pages[u - 1][:].indirect(n4_list[:]), nws[u - 1][:], COPY)
+                nc.sync.dma_start(out[P * (u - 1) : P * u, :], pages[u - 1][:])
+        nc.scalar.activation(pages[TILES - 1][:].indirect(n4_list[:]), nws[TILES - 1][:], COPY)
+        nc.sync.dma_start(out[P * (TILES - 1) :, :], pages[TILES - 1][:])

@@ -45,37 +45,24 @@ def tile_picked_pqhcrelaypagq_none_p_kernel(
             nc.sync.dma_start(tile[:].bitcast(I32), src[0].rearrange("p n t -> p (n t)").bitcast(I32))
             return tile
 
-        def load_scale_rows(queue, table, rows, first, step):
-            n = rows.shape[1]
-            picked = rows[first:16:step, :]
-            count = picked.shape[0]
-            queue.dma_start(
-                table[first:P:step, :].bitcast(I32),
-                picked.unsqueeze(1).to_broadcast([count, P // step // count, n]),
-            )
+        def load_scale_rows(name, src, width):
+            tile = keep.tile([P, width], U8, name=name, align_bytes=64)
+            rows = src[0].bitcast(I32)
+            nc.sync.dma_start(tile[:].bitcast(I32), rows.unsqueeze(1).to_broadcast([16, 8, width // 4]))
+            return tile
 
-        def place_odd_rows(dst, src):
-            for c, queue in enumerate((nc.scalar, nc.scalar)):
-                queue.dma_start(dst[2 + c : P : QUAD, :].bitcast(I32), src[GROUP + c : P : QUAD, :].bitcast(I32))
+        def place_rows(queue, plane):
+            for r in range(1, 4):
+                queue.dma_start(plane[r:P:QUAD, :].bitcast(I32), plane[8 * r : P : QUAD, :].bitcast(I32))
 
-        def place_odd_rows4(dst, src):
-            for c, queue in enumerate((nc.sync, nc.sync)):
-                queue.dma_start(dst[2 + c : P : QUAD, :].bitcast(I32), src[GROUP + 2 + c : P : QUAD, :].bitcast(I32))
-
-        d_byte_table = keep.tile([P, G], U8, name="d_byte_table", align_bytes=64)
-        x_byte_table = keep.tile([P, T], U8, name="x_byte_table", align_bytes=64)
-        d_rows = d_scales[0].bitcast(I32)
-        x_rows = x_scales[0].bitcast(I32)
-        k1_list = load_list("k1_list", k1)
-        load_scale_rows(nc.scalar, d_byte_table, d_rows, 0, 2)
-        load_scale_rows(nc.sync, d_byte_table, d_rows, 1, 2)
         offs_list = load_list("offs_list", offs)
-        d_word_table = load_words("d_word_table", d_words, G)
-        x_word_table = load_words("x_word_table", x_words, T)
-        for r in range(4):
-            load_scale_rows(nc.scalar, x_byte_table, x_rows, r, 4)
+        x_byte_table = load_scale_rows("x_byte_table", x_scales, T)
+        k1_list = load_list("k1_list", k1)
+        d_byte_table = load_scale_rows("d_byte_table", d_scales, G)
         n1_list = load_list("n1_list", n1)
         cand_list = load_list("cand_list", cand)
+        d_word_table = load_words("d_word_table", d_words, G)
+        x_word_table = load_words("x_word_table", x_words, T)
         n2_list = load_list("n2_list", n2)
         n3_list = load_list("n3_list", n3)
         n5_list = load_list("n5_list", n5)
@@ -89,16 +76,19 @@ def tile_picked_pqhcrelaypagq_none_p_kernel(
             nc.gpsimd.memset(s_row[:, S:], 0.0)
             s_rows.append(s_row)
 
+        planes = keep.tile([P, H + S], U8, name="planes", tag="d_plane", align_bytes=64)
+        d_plane = planes[:, :H]
+        q_plane = planes[:, H:]
+        q_bytes = keep.tile([P, S], U8, name="q_bytes", align_bytes=64)
+        nc.vector.tensor_copy(q_bytes[:], x_byte_table[:].indirect(offs_list[:]))
         d_bytes = keep.tile([P, H], U8, name="d_bytes", align_bytes=64)
         nc.vector.tensor_copy(d_bytes[:], d_byte_table[:].indirect(k1_list[:]))
-        d_plane = keep.tile([P, H], U8, name="d_plane", tag="d_plane", align_bytes=64)
+        nc.vector.tensor_copy(q_plane.bitcast(I32), q_bytes[:].bitcast(I32))
         nc.vector.tensor_copy(
-            d_plane[:].rearrange("p (t m) -> p m t", t=PACK),
+            d_plane.rearrange("p (t m) -> p m t", t=PACK),
             d_bytes[:].rearrange("p (m t) -> p m t", t=PACK),
         )
-        place_odd_rows(d_plane, d_plane)
-        q_plane = keep.tile([P, S], U8, name="q_plane", align_bytes=64)
-        nc.vector.tensor_copy(q_plane[:], x_byte_table[:].indirect(offs_list[:]))
+        place_rows(nc.scalar, planes)
         d_picked = keep.tile([P, H], U32, name="d_picked", tag="picked", align_bytes=64)
         nc.vector.tensor_copy(d_picked[:], d_word_table[:].indirect(k1_list[:]))
         d_codes = keep.tile([P, H], U32, name="d_codes", tag="stationary", align_bytes=64)
@@ -125,7 +115,7 @@ def tile_picked_pqhcrelaypagq_none_p_kernel(
                 lhsT=d_codes[:, cols].bitcast(FP8X4),
                 lhsT_scale=d_plane[:, cols],
                 rhs=q_codes[:].bitcast(FP8X4),
-                rhs_scale=q_plane[:],
+                rhs_scale=q_plane,
                 start=True,
                 stop=True,
             )
@@ -150,17 +140,19 @@ def tile_picked_pqhcrelaypagq_none_p_kernel(
         nc.vector.tensor_copy(cand_bytes[:], x_byte_table[:].indirect(cand_list[:]))
         cand_plane = keep.tile([P, C], U8, name="cand_plane", align_bytes=64)
         nc.vector.tensor_copy(cand_plane[:].bitcast(I32), cand_bytes[:].bitcast(I32))
-        place_odd_rows4(cand_plane, cand_bytes)
+        place_rows(nc.sync, cand_plane)
         cand_codes = keep.tile([P, C], U32, name="cand_codes", tag="stationary", align_bytes=64)
         nc.vector.tensor_copy(cand_codes[:], x_word_table[:].indirect(cand_list[:]))
 
         s_sums = [psum.tile([P, S], F32, name="s_sum%d" % u) for u in range(TILES)]
         pages = [keep.tile([P, U], F32, name="page%d" % u) for u in range(TILES)]
-        for lo, hi in CHUNKS:
+        for c, (lo, hi) in enumerate(CHUNKS):
             cols = slice(lo, hi)
             width = hi - lo
-            larger = keep.tile([P, TILES, width], F32, name="larger%d" % lo)
-            z = keep.tile([P, width, PACK], BF16, name="z%d" % lo, align_bytes=64)
+            if c < 2:
+                wide = keep.tile([P, TILES, S], F32, name="larger%d" % lo, tag="stage%d" % c, align_bytes=64)
+            larger = wide[:, :, cols]
+            z = keep.tile([P, width, PACK], BF16, name="z%d" % lo, tag="stage%d" % (2 * c + 1), align_bytes=64)
             for pair in ((0, 1), (2, 3)):
                 for t in pair:
                     nc.vector.scalar_tensor_tensor(

@@ -17,13 +17,17 @@ ALU = mybir.AluOpType
 
 P = 128
 PACK = 4
+BLOCK = 8
 GROUP = 16
 QUAD = 32
 TILES = 4
-CHUNKS = ((0, 64), (64, 128), (128, 256))
+SIXTEENTH = 0.0625
 DS_WIDTH = 384
 S_WIDTH = S + 8
-SIXTEENTH = 0.0625
+LEAD = 64
+CHUNKS = tuple((lo, lo + LEAD) for lo in range(0, S, LEAD))
+FETCHES = ((0, LEAD), (LEAD, 2 * LEAD), (2 * LEAD, S))
+LARGER_TAGS = ("larger0", "z0", "z_codes0")
 
 
 def tile_picked_pqhcrelaypagq_none_p_kernel(
@@ -45,20 +49,25 @@ def tile_picked_pqhcrelaypagq_none_p_kernel(
             nc.sync.dma_start(tile[:].bitcast(I32), src[0].rearrange("p n t -> p (n t)").bitcast(I32))
             return tile
 
-        def load_scale_rows(name, src, width):
+        def load_byte_table(name, src, width):
             tile = keep.tile([P, width], U8, name=name, align_bytes=64)
             rows = src[0].bitcast(I32)
-            nc.sync.dma_start(tile[:].bitcast(I32), rows.unsqueeze(1).to_broadcast([16, 8, width // 4]))
+            nc.sync.dma_start(
+                tile[:].bitcast(I32), rows.unsqueeze(1).to_broadcast([P // BLOCK, BLOCK, width // PACK])
+            )
             return tile
 
         def place_rows(queue, plane):
-            for r in range(1, 4):
-                queue.dma_start(plane[r:P:QUAD, :].bitcast(I32), plane[8 * r : P : QUAD, :].bitcast(I32))
+            for r in range(1, QUAD // BLOCK):
+                queue.dma_start(plane[r:P:QUAD, :].bitcast(I32), plane[BLOCK * r : P : QUAD, :].bitcast(I32))
+
+        def entries(list_tile, lo, hi):
+            return list_tile[:, lo // GROUP : hi // GROUP]
 
         offs_list = load_list("offs_list", offs)
-        x_byte_table = load_scale_rows("x_byte_table", x_scales, T)
+        x_byte_table = load_byte_table("x_byte_table", x_scales, T)
         k1_list = load_list("k1_list", k1)
-        d_byte_table = load_scale_rows("d_byte_table", d_scales, G)
+        d_byte_table = load_byte_table("d_byte_table", d_scales, G)
         n1_list = load_list("n1_list", n1)
         cand_list = load_list("cand_list", cand)
         d_word_table = load_words("d_word_table", d_words, G)
@@ -76,7 +85,7 @@ def tile_picked_pqhcrelaypagq_none_p_kernel(
             nc.gpsimd.memset(s_row[:, S:], 0.0)
             s_rows.append(s_row)
 
-        planes = keep.tile([P, H + S], U8, name="planes", tag="d_plane", align_bytes=64)
+        planes = keep.tile([P, H + S], U8, name="planes", tag="planes", align_bytes=64)
         d_plane = planes[:, :H]
         q_plane = planes[:, H:]
         q_bytes = keep.tile([P, S], U8, name="q_bytes", align_bytes=64)
@@ -101,11 +110,10 @@ def tile_picked_pqhcrelaypagq_none_p_kernel(
 
         h_sums = []
         ds_rows = []
-        lead = CHUNKS[0][1]
-        gots = {}
+        fetched = {}
 
         def fetch_ds(dst, t, lo, hi):
-            nc.scalar.activation(dst, ds_rows[t][:, :S].indirect(n2_list[:, lo // GROUP : hi // GROUP]), COPY)
+            nc.scalar.activation(dst, ds_rows[t][:, :S].indirect(entries(n2_list, lo, hi)), COPY)
 
         for t in range(TILES):
             cols = slice(P * t, P * (t + 1))
@@ -126,17 +134,19 @@ def tile_picked_pqhcrelaypagq_none_p_kernel(
             h_sums.append(h_sum)
             ds_rows.append(ds_row)
             if 0 < t < TILES - 1:
-                early = keep.tile([P, lead], F32, name="early%d" % t, tag="h_row%d" % t)
-                fetch_ds(early[:], t - 1, 0, lead)
-                gots[(t - 1, 0)] = early[:]
+                early = keep.tile([P, LEAD], F32, name="early%d" % t, tag="h_row%d" % t)
+                fetch_ds(early[:], t - 1, 0, LEAD)
+                fetched[(t - 1, 0)] = early[:]
         late = keep.tile([P, TILES, S], F32, name="late", tag="h_row%d" % (TILES - 1))
+        for lo, hi in FETCHES:
+            for t in range(TILES):
+                if (t, lo) not in fetched:
+                    fetch_ds(late[:, t, lo:hi], t, lo, hi)
         for lo, hi in CHUNKS:
             for t in range(TILES):
-                if (t, lo) not in gots:
-                    fetch_ds(late[:, t, lo:hi], t, lo, hi)
-                    gots[(t, lo)] = late[:, t, lo:hi]
+                fetched.setdefault((t, lo), late[:, t, lo:hi])
 
-        cand_bytes = keep.tile([P, C], U8, name="cand_bytes", tag="d_plane", align_bytes=64)
+        cand_bytes = keep.tile([P, C], U8, name="cand_bytes", tag="planes", align_bytes=64)
         nc.vector.tensor_copy(cand_bytes[:], x_byte_table[:].indirect(cand_list[:]))
         cand_plane = keep.tile([P, C], U8, name="cand_plane", align_bytes=64)
         nc.vector.tensor_copy(cand_plane[:].bitcast(I32), cand_bytes[:].bitcast(I32))
@@ -149,18 +159,18 @@ def tile_picked_pqhcrelaypagq_none_p_kernel(
         for c, (lo, hi) in enumerate(CHUNKS):
             cols = slice(lo, hi)
             width = hi - lo
-            if c < 2:
-                wide = keep.tile([P, TILES, S], F32, name="larger%d" % lo, tag="stage%d" % c, align_bytes=64)
+            if c < len(LARGER_TAGS):
+                wide = keep.tile([P, TILES, S], F32, name="larger%d" % lo, tag=LARGER_TAGS[c], align_bytes=64)
             larger = wide[:, :, cols]
-            z = keep.tile([P, width, PACK], BF16, name="z%d" % lo, tag="stage%d" % (2 * c + 1), align_bytes=64)
+            z = keep.tile([P, width, PACK], BF16, name="z%d" % lo, tag="z%d" % c, align_bytes=64)
             for pair in ((0, 1), (2, 3)):
                 for t in pair:
                     nc.vector.scalar_tensor_tensor(
-                        larger[:, t, :], h_sums[t][:, cols], SIXTEENTH, gots[(t, lo)], ALU.mult, ALU.max
+                        larger[:, t, :], h_sums[t][:, cols], SIXTEENTH, fetched[(t, lo)], ALU.mult, ALU.max
                     )
                 for t in pair:
                     nc.vector.tensor_scalar(z[:, :, t], larger[:, t, :], gain[:, t : t + 1], None, ALU.mult)
-            z_codes = keep.tile([P, width], U32, name="z_codes%d" % lo, align_bytes=64)
+            z_codes = keep.tile([P, width], U32, name="z_codes%d" % lo, tag="z_codes%d" % c, align_bytes=64)
             z_plane = keep.tile([P, width], U8, name="z_plane%d" % lo, align_bytes=64)
             nc.vector.quantize_mx(
                 out=z_codes[:].bitcast(FP8X4), scales=z_plane[:], in_=z[:].rearrange("p j t -> p (j t)")
@@ -179,7 +189,11 @@ def tile_picked_pqhcrelaypagq_none_p_kernel(
                 nc.vector.tensor_scalar(s_rows[u][:, cols], s_sums[u][:, cols], SIXTEENTH, None, ALU.mult)
 
         def put_s(u, lo, hi):
-            nc.scalar.activation(pages[u][:].indirect(n3_list[:, lo // GROUP : hi // GROUP]), s_rows[u][:, lo:hi], COPY)
+            nc.scalar.activation(pages[u][:].indirect(entries(n3_list, lo, hi)), s_rows[u][:, lo:hi], COPY)
+
+        def put_nw_and_store(u, nw):
+            nc.scalar.activation(pages[u][:].indirect(n4_list[:]), nw[:], COPY)
+            nc.sync.dma_start(out[P * u : P * (u + 1), :], pages[u][:])
 
         for lo, hi in CHUNKS[:-1]:
             for u in range(TILES):
@@ -193,7 +207,5 @@ def tile_picked_pqhcrelaypagq_none_p_kernel(
             nws.append(nw)
             put_s(u, CHUNKS[-1][0], CHUNKS[-1][1])
             if u > 0:
-                nc.scalar.activation(pages[u - 1][:].indirect(n4_list[:]), nws[u - 1][:], COPY)
-                nc.sync.dma_start(out[P * (u - 1) : P * u, :], pages[u - 1][:])
-        nc.scalar.activation(pages[TILES - 1][:].indirect(n4_list[:]), nws[TILES - 1][:], COPY)
-        nc.sync.dma_start(out[P * (TILES - 1) :, :], pages[TILES - 1][:])
+                put_nw_and_store(u - 1, nws[u - 1])
+        put_nw_and_store(TILES - 1, nws[TILES - 1])

from contextlib import ExitStack

import concourse.mybir as mybir

K, T, S, G, H, C, U = 512, 1024, 256, 2048, 512, 512, 512
FLOPS = 2 * K * H * S + 2 * K * C * S

F32 = mybir.dt.float32
BF16 = mybir.dt.bfloat16
I32 = mybir.dt.int32
U32 = mybir.dt.uint32
U16 = mybir.dt.uint16
U8 = mybir.dt.uint8
FP8X4 = mybir.dt.float8_e4m3fn_x4
COPY = mybir.ActivationFunctionType.Copy
ALU = mybir.AluOpType

P = 128
PACK = 4
BLOCK = 8
GROUP = 16
QUAD = 32
TILES = 4
SIXTEENTH = 0.0625
DS_WIDTH = 384
S_WIDTH = S + 8
LEAD = 64
CHUNKS = tuple((lo, lo + LEAD) for lo in range(0, S, LEAD))
FETCHES = ((0, LEAD), (LEAD, 2 * LEAD), (2 * LEAD, S))
LARGER_TAGS = ("larger0", "z0", "z_codes0")


def tile_picked_pqhcrelaypagq_none_p_kernel(
    tc, x_words, x_scales, d_words, d_scales, gs, offs, k1, n1, n2, cand, n3, n4, n5, out
):
    nc = tc.nc
    with ExitStack() as ctx:
        lists = ctx.enter_context(tc.tile_pool(name="lists", bufs=1))
        keep = ctx.enter_context(tc.tile_pool(name="keep", bufs=1))
        psum = ctx.enter_context(tc.psum_pool(name="psum", bufs=1))

        def load_list(name, src):
            tile = lists.tile(list(src.shape), U16, name=name)
            nc.sync.dma_start(tile[:], src)
            return tile

        def load_words(name, src, width):
            tile = keep.tile([P, width], U32, name=name, align_bytes=64)
            nc.sync.dma_start(tile[:].bitcast(I32), src[0].rearrange("p n t -> p (n t)").bitcast(I32))
            return tile

        def load_byte_table(name, src, width):
            tile = keep.tile([P, width], U8, name=name, align_bytes=64)
            rows = src[0].bitcast(I32)
            nc.sync.dma_start(
                tile[:].bitcast(I32), rows.unsqueeze(1).to_broadcast([P // BLOCK, BLOCK, width // PACK])
            )
            return tile

        def place_rows(queue, plane):
            for r in range(1, QUAD // BLOCK):
                queue.dma_start(plane[r:P:QUAD, :].bitcast(I32), plane[BLOCK * r : P : QUAD, :].bitcast(I32))

        def entries(list_tile, lo, hi):
            return list_tile[:, lo // GROUP : hi // GROUP]

        offs_list = load_list("offs_list", offs)
        x_byte_table = load_byte_table("x_byte_table", x_scales, T)
        k1_list = load_list("k1_list", k1)
        d_byte_table = load_byte_table("d_byte_table", d_scales, G)
        n1_list = load_list("n1_list", n1)
        cand_list = load_list("cand_list", cand)
        d_word_table = load_words("d_word_table", d_words, G)
        x_word_table = load_words("x_word_table", x_words, T)
        n2_list = load_list("n2_list", n2)
        n3_list = load_list("n3_list", n3)
        n5_list = load_list("n5_list", n5)
        n4_list = load_list("n4_list", n4)
        gain = keep.tile([P, PACK], F32, name="gain")
        nc.gpsimd.dma_start(gain[:], gs.rearrange("(p t) o -> p (t o)", t=PACK))

        s_rows = []
        for u in range(TILES):
            s_row = keep.tile([P, S_WIDTH], F32, name="s_row%d" % u)
            nc.gpsimd.memset(s_row[:, S:], 0.0)
            s_rows.append(s_row)

        planes = keep.tile([P, H + S], U8, name="planes", tag="planes", align_bytes=64)
        d_plane = planes[:, :H]
        q_plane = planes[:, H:]
        q_bytes = keep.tile([P, S], U8, name="q_bytes", align_bytes=64)
        nc.vector.tensor_copy(q_bytes[:], x_byte_table[:].indirect(offs_list[:]))
        d_bytes = keep.tile([P, H], U8, name="d_bytes", align_bytes=64)
        nc.vector.tensor_copy(d_bytes[:], d_byte_table[:].indirect(k1_list[:]))
        nc.vector.tensor_copy(q_plane.bitcast(I32), q_bytes[:].bitcast(I32))
        nc.vector.tensor_copy(
            d_plane.rearrange("p (t m) -> p m t", t=PACK),
            d_bytes[:].rearrange("p (m t) -> p m t", t=PACK),
        )
        place_rows(nc.scalar, planes)
        d_picked = keep.tile([P, H], U32, name="d_picked", tag="picked", align_bytes=64)
        nc.vector.tensor_copy(d_picked[:], d_word_table[:].indirect(k1_list[:]))
        d_codes = keep.tile([P, H], U32, name="d_codes", tag="stationary", align_bytes=64)
        nc.vector.tensor_copy(
            d_codes[:].rearrange("p (t m) -> p m t", t=PACK),
            d_picked[:].rearrange("p (m t) -> p m t", t=PACK),
        )
        q_codes = keep.tile([P, S], U32, name="q_codes", tag="picked", align_bytes=64)
        nc.vector.tensor_copy(q_codes[:], x_word_table[:].indirect(offs_list[:]))

        h_sums = []
        ds_rows = []
        fetched = {}

        def fetch_ds(dst, t, lo, hi):
            nc.scalar.activation(dst, ds_rows[t][:, :S].indirect(entries(n2_list, lo, hi)), COPY)

        for t in range(TILES):
            cols = slice(P * t, P * (t + 1))
            h_sum = psum.tile([P, S], F32, name="h_sum%d" % t)
            nc.tensor.matmul_mx(
                out=h_sum[:],
                lhsT=d_codes[:, cols].bitcast(FP8X4),
                lhsT_scale=d_plane[:, cols],
                rhs=q_codes[:].bitcast(FP8X4),
                rhs_scale=q_plane,
                start=True,
                stop=True,
            )
            h_row = keep.tile([P, S], F32, name="h_row%d" % t, tag="h_row%d" % t)
            nc.vector.tensor_scalar(h_row[:], h_sum[:], SIXTEENTH, None, ALU.mult)
            ds_row = keep.tile([P, DS_WIDTH], F32, name="ds_row%d" % t)
            nc.scalar.activation(ds_row[:].indirect(n1_list[:]), h_row[:], COPY)
            h_sums.append(h_sum)
            ds_rows.append(ds_row)
            if 0 < t < TILES - 1:
                early = keep.tile([P, LEAD], F32, name="early%d" % t, tag="h_row%d" % t)
                fetch_ds(early[:], t - 1, 0, LEAD)
                fetched[(t - 1, 0)] = early[:]
        late = keep.tile([P, TILES, S], F32, name="late", tag="h_row%d" % (TILES - 1))
        for lo, hi in FETCHES:
            for t in range(TILES):
                if (t, lo) not in fetched:
                    fetch_ds(late[:, t, lo:hi], t, lo, hi)
        for lo, hi in CHUNKS:
            for t in range(TILES):
                fetched.setdefault((t, lo), late[:, t, lo:hi])

        cand_bytes = keep.tile([P, C], U8, name="cand_bytes", tag="planes", align_bytes=64)
        nc.vector.tensor_copy(cand_bytes[:], x_byte_table[:].indirect(cand_list[:]))
        cand_plane = keep.tile([P, C], U8, name="cand_plane", align_bytes=64)
        nc.vector.tensor_copy(cand_plane[:].bitcast(I32), cand_bytes[:].bitcast(I32))
        place_rows(nc.sync, cand_plane)
        cand_codes = keep.tile([P, C], U32, name="cand_codes", tag="stationary", align_bytes=64)
        nc.vector.tensor_copy(cand_codes[:], x_word_table[:].indirect(cand_list[:]))

        s_sums = [psum.tile([P, S], F32, name="s_sum%d" % u) for u in range(TILES)]
        pages = [keep.tile([P, U], F32, name="page%d" % u) for u in range(TILES)]
        for c, (lo, hi) in enumerate(CHUNKS):
            cols = slice(lo, hi)
            width = hi - lo
            if c < len(LARGER_TAGS):
                wide = keep.tile([P, TILES, S], F32, name="larger%d" % lo, tag=LARGER_TAGS[c], align_bytes=64)
            larger = wide[:, :, cols]
            z = keep.tile([P, width, PACK], BF16, name="z%d" % lo, tag="z%d" % c, align_bytes=64)
            for pair in ((0, 1), (2, 3)):
                for t in pair:
                    nc.vector.scalar_tensor_tensor(
                        larger[:, t, :], h_sums[t][:, cols], SIXTEENTH, fetched[(t, lo)], ALU.mult, ALU.max
                    )
                for t in pair:
                    nc.vector.tensor_scalar(z[:, :, t], larger[:, t, :], gain[:, t : t + 1], None, ALU.mult)
            z_codes = keep.tile([P, width], U32, name="z_codes%d" % lo, tag="z_codes%d" % c, align_bytes=64)
            z_plane = keep.tile([P, width], U8, name="z_plane%d" % lo, align_bytes=64)
            nc.vector.quantize_mx(
                out=z_codes[:].bitcast(FP8X4), scales=z_plane[:], in_=z[:].rearrange("p j t -> p (j t)")
            )
            for u in range(TILES):
                rows = slice(P * u, P * (u + 1))
                nc.tensor.matmul_mx(
                    out=s_sums[u][:, cols],
                    lhsT=cand_codes[:, rows].bitcast(FP8X4),
                    lhsT_scale=cand_plane[:, rows],
                    rhs=z_codes[:].bitcast(FP8X4),
                    rhs_scale=z_plane[:],
                    start=True,
                    stop=True,
                )
                nc.vector.tensor_scalar(s_rows[u][:, cols], s_sums[u][:, cols], SIXTEENTH, None, ALU.mult)

        def put_s(u, lo, hi):
            nc.scalar.activation(pages[u][:].indirect(entries(n3_list, lo, hi)), s_rows[u][:, lo:hi], COPY)

        def put_nw_and_store(u, nw):
            nc.scalar.activation(pages[u][:].indirect(n4_list[:]), nw[:], COPY)
            nc.sync.dma_start(out[P * u : P * (u + 1), :], pages[u][:])

        for lo, hi in CHUNKS[:-1]:
            for u in range(TILES):
                put_s(u, lo, hi)
        nws = []
        for u in range(TILES):
            other = keep.tile([P, S], F32, name="other%d" % u)
            nc.scalar.activation(other[:], s_rows[u][:].indirect(n5_list[:]), COPY)
            nw = keep.tile([P, S], F32, name="nw%d" % u)
            nc.vector.tensor_tensor(nw[:], s_rows[u][:, :S], other[:], ALU.subtract)
            nws.append(nw)
            put_s(u, CHUNKS[-1][0], CHUNKS[-1][1])
            if u > 0:
                put_nw_and_store(u - 1, nws[u - 1])
        put_nw_and_store(TILES - 1, nws[TILES - 1])
